import numpy as np, ml_dtypes
CORES = [51,54,179,182]
N = 4
import mx_ref
NC, G = 128, 4
EPS = 0.001
BF = ml_dtypes.bfloat16
def cut(t, i, w=512):
    return t[:, w * i:w * i + w]
def tile(rs):
    return np.stack(rs, axis=2).reshape(128, -1).astype(BF)
def layer(w, X):
    out = []
    for i in range(G):
        for t in range(len(X)):
            p = mx_ref.matmul(mx_ref.quantize(cut(w, len(X) * i + t)), X[t])
            z = p if t == 0 else z + p
        out.append(z)
    return out
def normed(Z, s):
    return [z * f for z, f in zip(Z, s)]
def setup_inputs(rng):
    def f(*shape):
        return mx_ref.flush((rng.standard_normal(shape, dtype=np.float32) * np.exp2(rng.integers(-2, 3, shape[:-1] + (1,)))).astype(BF))
    return {"x": f(N, 128, 4 * NC), "w1": f(N, 128, G * 512), "w2": f(N, 128, 2 * 512)}
def setup_inputs_blocks(rng):
    d = setup_inputs(rng)
    for k in ("x", "w1", "w2"): d[k] = mx_ref.spread(d[k], rng, 4)
    return d
def setup_inputs_wide(rng):
    d = setup_inputs(rng)
    for k in ("x", "w1", "w2"): d[k] = mx_ref.flush((d[k].astype(np.float32) * np.exp2(rng.integers(-5, 6, (N, 1, 1))).astype(np.float32)).astype(BF))
    return d
def setup_inputs_rows(rng):
    d = setup_inputs(rng); v = d["w1"].astype(np.float32).reshape(N, 128, -1, 4)
    d["w1"] = mx_ref.flush((v * np.exp2(rng.integers(-6, 7, (N, 1, v.shape[2], 1))).astype(np.float32)).reshape(d["w1"].shape).astype(BF))
    return d
def setup_inputs_faint(rng):
    d = setup_inputs(rng); d["x"] = mx_ref.flush((d["x"].astype(np.float32) * np.float32(2.0 ** -12)).astype(BF))
    return d
def reference(x, w1, w2, own=None):
    Z = [layer(w1[r], [mx_ref.quantize(x[r])]) for r in range(N)]
    ms = [sum((Z[r][i].astype(np.float64) ** 2).sum(axis=1, keepdims=True) for r in range(N)) / (N * NC) for i in range(G)]
    s = [(1 / np.sqrt(m + EPS)).astype(np.float32) for m in ms]
    h = np.stack([tile(normed(Z[r], s)) for r in range(N)])
    use = h if own is None else own["h"]
    H = [mx_ref.quantize(use[j]) for j in range(N)]
    y = np.zeros((N, 128, NC), np.float32)
    for r in range(N):
        y[r] = mx_ref.matmul(mx_ref.quantize(cut(w2[r], 0)), H[r]) + mx_ref.matmul(mx_ref.quantize(cut(w2[r], 1)), H[(r + 1) % N])
    return {"h": h, "y": y}

@@ -1,0 +1,177 @@
+import numpy
+from concourse.bass import DstId, RemoteDMATransfer
+from concourse.mybir import dt, AluOpType, ActivationFunctionType
+
+N, NC, G, EPS = 4, 128, 4, 0.001
+TW = 4 * NC
+CHUNKS = ((0, 1), (1, 4))
+LOADS = ((0, 1), (1, 3), (3, 4))
+SPLIT_FIRST = True
+
+F32, BF16, CODE, U8 = "float32", "bfloat16", "float8_e4m3fn_x4", "uint8"
+SCRATCH = {
+    "xb": ("sbuf", [128, TW], BF16), "qx": ("sbuf", [128, NC], CODE), "sx": ("sbuf", [128, NC], U8),
+    "w1b": ("sbuf", [128, G * TW], BF16), "qw1": ("sbuf", [128, G * NC], CODE), "sw1": ("sbuf", [128, G * NC], U8),
+    "w2b": ("sbuf", [128, 2 * TW], BF16), "qw2": ("sbuf", [128, 2 * NC], CODE), "sw2": ("sbuf", [128, 2 * NC], U8),
+    "hb": ("sbuf", [128, TW], BF16), "qh": ("sbuf", [128, NC], CODE), "sh": ("sbuf", [128, NC], U8),
+    "qr": ("sbuf", [128, NC], CODE), "sr": ("sbuf", [128, NC], U8),
+    "sq": ("sbuf", [128, G * NC], F32),
+    "yb": ("sbuf", [128, NC], F32),
+    "z": ("psum", [128, G * 512], F32), "yp": ("psum", [128, 512], F32),
+}
+SEMAPHORES = ["lx", "lsecond", "vx", "vsecond", "vc", "nS", "nV", "vh", "harr", "my", "yc", "sth", "sty", "sent", "sentH"]
+for _k in range(len(LOADS)):
+    SEMAPHORES.append("lfirst%d" % _k)
+for _i in range(G):
+    SEMAPHORES += ["vw%d" % _i, "mm%d" % _i]
+for _c, (_a, _b) in enumerate(CHUNKS):
+    for _n in ("own", "pre", "prn", "far", "tot", "rec", "s"):
+        SCRATCH["%s%d" % (_n, _c)] = ("sbuf", [128, _b - _a], F32)
+    SCRATCH["land%d" % _c] = ("sbuf", [128, (N - 1) * (_b - _a)], F32)
+    SEMAPHORES += ["a%d" % _c, "on%d" % _c, "off%d" % _c, "r%d" % _c, "sd%d" % _c]
+
+
+def _bits(m):
+    return [e for e in range(m.bit_length()) if (m >> e) & 1]
+
+
+def _mask(es):
+    return sum(1 << e for e in es)
+
+
+def _peers(c, cores, topo):
+    o = [d for d in cores if d != c]
+    near = [d for d in o if topo.host(d) == topo.host(c) and topo.chip(d) == topo.chip(c)]
+    return near, [d for d in o if d not in near]
+
+
+def rank_program(g, core, T, topo):
+    rank = T.rank_of(core)
+    if rank is None:
+        return
+    V, S, P, Y, sem = g.vector, g.scalar, g.tensor, g.sync, T.sem
+    AF, OP = ActivationFunctionType, AluOpType
+    cores = list(T.cores)
+    near, far = _peers(core, cores, topo)
+    far_e = _bits(topo.mask(core, far[0]))
+    near_e = [e for e in _bits(topo.mask(core, near[0])) if e not in far_e]
+    half = len(far_e) // len(far)
+    eng = {near[0]: near_e}
+    for k, d in enumerate(far):
+        eng[d] = far_e[k * half:(k + 1) * half]
+    n_on, n_off = len(near_e), half * len(far)
+
+    def zb(i):
+        return T.z[:, 512 * i:512 * i + NC]
+
+    def chunk_of(i):
+        for c, (a, b) in enumerate(CHUNKS):
+            if a <= i < b:
+                return c, i - a
+
+    Y.dma_start(T.xb[:], T.x[:]).then_inc(sem.lx, 16)
+    for k, (a, b) in enumerate(LOADS):
+        q = S if k == 0 else Y
+        q.dma_start(T.w1b[:, TW * a:TW * b], T.w1[:, TW * a:TW * b]).then_inc(sem["lfirst%d" % k], 16)
+
+    V.wait_ge(sem.lx, 16)
+    V.quantize_mx(T.qx[:], T.sx[:], T.xb[:]).then_inc(sem.vx, 1)
+    P.wait_ge(sem.vx, 1)
+    for k, (a, b) in enumerate(LOADS):
+        V.wait_ge(sem["lfirst%d" % k], 16)
+        for i in range(a, b):
+            V.quantize_mx(T.qw1[:, NC * i:NC * i + NC], T.sw1[:, NC * i:NC * i + NC],
+                          T.w1b[:, TW * i:TW * i + TW]).then_inc(sem["vw%d" % i], 1)
+            P.wait_ge(sem["vw%d" % i], 1)
+            P.matmul_mx(zb(i), T.qw1[:, NC * i:NC * i + NC], T.sw1[:, NC * i:NC * i + NC], T.qx[:], T.sx[:],
+                        True, True).then_inc(sem["mm%d" % i], 1)
+            c, j = chunk_of(i)
+            S.wait_ge(sem["mm%d" % i], 1)
+            S.activation(T.sq[:, NC * i:NC * i + NC], zb(i), AF.Square,
+                         accum_out=T["own%d" % c][:, j:j + 1]).then_inc(sem["a%d" % c], 1)
+
+    sent = 0
+    for c, (a, b) in enumerate(CHUNKS):
+        w = b - a
+        tr = {}
+        for d in near + far:
+            dn, df = _peers(d, cores, topo)
+            slot = (dn + df).index(core)
+            rid, pid = topo.addr(d, core)
+            tr[d] = RemoteDMATransfer(dst_ids=[DstId(rid=rid, pnc=pid)], dma_engine_mask=_mask(eng[d]),
+                                      remote_sem=sem[("on%d" if d in near else "off%d") % c],
+                                      src=T["own%d" % c][:], dst=T["land%d" % c][:, slot * w:slot * w + w])
+            sent += len(eng[d])
+        g.wait_ge(sem["a%d" % c], w)
+        if c == 0 and SPLIT_FIRST:
+            g.remote_dma_fused([tr[d] for d in far], local_sem=sem.sent)
+            g.remote_dma_fused([tr[d] for d in near], local_sem=sem.sent)
+        else:
+            g.remote_dma_fused([tr[d] for d in far + near], local_sem=sem.sent)
+
+    Y.wait_ge(sem.sent, sent)
+    Y.dma_start(T.w2b[:], T.w2[:]).then_inc(sem.lsecond, 16)
+
+    vc = [0]
+
+    def vstep(ins):
+        ins.then_inc(sem.vc, 1)
+        vc[0] += 1
+
+    shift = float(numpy.float32(EPS)) * (N * NC)
+    for c, (a, b) in enumerate(CHUNKS):
+        w = b - a
+        own, pre, prn, fr, tot, rec, land = (T["%s%d" % (n, c)] for n in ("own", "pre", "prn", "far", "tot", "rec", "land"))
+        V.wait_ge(sem["a%d" % c], w)
+        vstep(V.tensor_scalar(pre[:], own[:], shift, None, OP.add))
+        V.wait_ge(sem["on%d" % c], n_on)
+        V.wait_ge(sem.vc, vc[0])
+        vstep(V.tensor_tensor(prn[:], pre[:], land[:, 0:w], OP.add))
+        V.wait_ge(sem["off%d" % c], n_off)
+        vstep(V.tensor_tensor(fr[:], land[:, w:2 * w], land[:, 2 * w:3 * w], OP.add))
+        V.wait_ge(sem.vc, vc[0])
+        vstep(V.tensor_tensor(tot[:], fr[:], prn[:], OP.add))
+        V.wait_ge(sem.vc, vc[0])
+        V.reciprocal(rec[:], tot[:]).then_inc(sem["r%d" % c], 1)
+        S.wait_ge(sem["r%d" % c], 1)
+        S.activation(T["s%d" % c][:], rec[:], AF.Sqrt, scale=float(N * NC)).then_inc(sem["sd%d" % c], 1)
+
+    for i in range(G):
+        c, j = chunk_of(i)
+        col, out = T["s%d" % c][:, j:j + 1], T.hb[:, i:TW:4]
+        if i < G // 2:
+            V.wait_ge(sem["sd%d" % c], 1)
+            V.tensor_scalar(out, zb(i), col, None, OP.mult).then_inc(sem.nV, 1)
+        else:
+            S.wait_ge(sem["sd%d" % c], 1)
+            S.activation(out, zb(i), AF.Identity, scale=col).then_inc(sem.nS, 1)
+    V.wait_ge(sem.nV, G // 2)
+    V.wait_ge(sem.nS, G - G // 2)
+    V.quantize_mx(T.qh[:], T.sh[:], T.hb[:]).then_inc(sem.vh, 1)
+
+    dst, src = cores[(rank - 1) % N], cores[(rank + 1) % N]
+    rid, pid = topo.addr(dst, core)
+    m = topo.mask(core, dst)
+    g.wait_ge(sem.vh, 1)
+    g.remote_dma(T.qr[:].bitcast(dt.uint8), T.qh[:].bitcast(dt.uint8), sem.harr, sem.sentH, pid, rid, m)
+    g.remote_dma(T.sr[:], T.sh[:], sem.harr, sem.sentH, pid, rid, m)
+
+    V.wait_ge(sem.lsecond, 16)
+    for t in range(2):
+        V.quantize_mx(T.qw2[:, NC * t:NC * t + NC], T.sw2[:, NC * t:NC * t + NC],
+                      T.w2b[:, TW * t:TW * t + TW]).then_inc(sem.vsecond, 1)
+    P.wait_ge(sem.vh, 1)
+    P.wait_ge(sem.vsecond, 2)
+    P.matmul_mx(T.yp[:, 0:NC], T.qw2[:, 0:NC], T.sw2[:, 0:NC], T.qh[:], T.sh[:], True, False)
+    P.wait_ge(sem.harr, 2 * len(_bits(topo.mask(src, core))))
+    P.matmul_mx(T.yp[:, 0:NC], T.qw2[:, NC:2 * NC], T.sw2[:, NC:2 * NC], T.qr[:], T.sr[:], False, True).then_inc(sem.my, 1)
+    V.wait_ge(sem.my, 1)
+    V.tensor_copy(T.yb[:], T.yp[:, 0:NC]).then_inc(sem.yc, 1)
+
+    Y.wait_ge(sem.vh, 1)
+    Y.wait_ge(sem.sentH, 2 * len(_bits(m)))
+    Y.dma_start(T.h[:], T.hb[:]).then_inc(sem.sth, 16)
+    Y.wait_ge(sem.yc, 1)
+    Y.dma_start(T.y[:], T.yb[:]).then_inc(sem.sty, 16)
+    Y.wait_ge(sem.sth, 16)
+    Y.wait_ge(sem.sty, 16)

@@ -1,12 +1,12 @@
 import numpy
 from concourse.bass import DstId, RemoteDMATransfer
-from concourse.mybir import dt, AluOpType, ActivationFunctionType
+from concourse.mybir import dt, AluOpType, AxisListType, ActivationFunctionType
 
 N, NC, G, EPS = 4, 128, 4, 0.001
 TW = 4 * NC
 CHUNKS = ((0, 1), (1, 4))
 LOADS = ((0, 1), (1, 3), (3, 4))
-SPLIT_FIRST = True
+BLK = 4
 
 F32, BF16, CODE, U8 = "float32", "bfloat16", "float8_e4m3fn_x4", "uint8"
 SCRATCH = {
@@ -17,18 +17,22 @@ SCRATCH = {
     "qr": ("sbuf", [128, NC], CODE), "sr": ("sbuf", [128, NC], U8),
     "sq": ("sbuf", [128, G * NC], F32),
     "yb": ("sbuf", [128, NC], F32),
+    "ra": ("sbuf", [128, 1], F32), "u": ("sbuf", [128, 1], F32), "v": ("sbuf", [128, 1], F32),
+    "pre0": ("sbuf", [128, 1], F32), "prn0": ("sbuf", [128, 1], F32), "far0": ("sbuf", [128, 1], F32),
+    "land0": ("sbuf", [128, N - 1], F32),
+    "land1": ("sbuf", [128, N * BLK], F32),
     "z": ("psum", [128, G * 512], F32), "yp": ("psum", [128, 512], F32),
 }
-SEMAPHORES = ["lx", "lsecond", "vx", "vsecond", "vc", "nS", "nV", "vh", "harr", "my", "yc", "sth", "sty", "sent", "sentH"]
+SEMAPHORES = ["lx", "lsecond", "vx", "vsecond", "vc", "nS", "nV", "vh", "harr", "my", "yc", "sth", "sty", "sent",
+              "sentC", "sentS", "ra", "sc", "h3a", "sd"]
 for _k in range(len(LOADS)):
     SEMAPHORES.append("lfirst%d" % _k)
 for _i in range(G):
     SEMAPHORES += ["vw%d" % _i, "mm%d" % _i]
 for _c, (_a, _b) in enumerate(CHUNKS):
-    for _n in ("own", "pre", "prn", "far", "tot", "rec", "s"):
+    for _n in ("own", "tot", "rec", "s"):
         SCRATCH["%s%d" % (_n, _c)] = ("sbuf", [128, _b - _a], F32)
-    SCRATCH["land%d" % _c] = ("sbuf", [128, (N - 1) * (_b - _a)], F32)
-    SEMAPHORES += ["a%d" % _c, "on%d" % _c, "off%d" % _c, "r%d" % _c, "sd%d" % _c]
+    SEMAPHORES += ["a%d" % _c, "on%d" % _c, "off%d" % _c, "r%d" % _c]
 
 
 def _bits(m):
@@ -53,13 +57,11 @@ def rank_program(g, core, T, topo):
     AF, OP = ActivationFunctionType, AluOpType
     cores = list(T.cores)
     near, far = _peers(core, cores, topo)
+    far.sort(key=lambda d: d in _peers(cores[(cores.index(d) - 1) % N], cores, topo)[0])
     far_e = _bits(topo.mask(core, far[0]))
     near_e = [e for e in _bits(topo.mask(core, near[0])) if e not in far_e]
-    half = len(far_e) // len(far)
-    eng = {near[0]: near_e}
-    for k, d in enumerate(far):
-        eng[d] = far_e[k * half:(k + 1) * half]
-    n_on, n_off = len(near_e), half * len(far)
+    n_on, n_off = len(near_e), len(far_e) * len(far)
+    W1 = CHUNKS[1][1] - CHUNKS[1][0]
 
     def zb(i):
         return T.z[:, 512 * i:512 * i + NC]
@@ -71,8 +73,7 @@ def rank_program(g, core, T, topo):
 
     Y.dma_start(T.xb[:], T.x[:]).then_inc(sem.lx, 16)
     for k, (a, b) in enumerate(LOADS):
-        q = S if k == 0 else Y
-        q.dma_start(T.w1b[:, TW * a:TW * b], T.w1[:, TW * a:TW * b]).then_inc(sem["lfirst%d" % k], 16)
+        Y.dma_start(T.w1b[:, TW * a:TW * b], T.w1[:, TW * a:TW * b]).then_inc(sem["lfirst%d" % k], 16)
 
     V.wait_ge(sem.lx, 16)
     V.quantize_mx(T.qx[:], T.sx[:], T.xb[:]).then_inc(sem.vx, 1)
@@ -93,68 +94,92 @@ def rank_program(g, core, T, topo):
     sent = 0
     for c, (a, b) in enumerate(CHUNKS):
         w = b - a
-        tr = {}
-        for d in near + far:
+        step = w if c == 0 else BLK
+
+        def place(d):
             dn, df = _peers(d, cores, topo)
             slot = (dn + df).index(core)
             rid, pid = topo.addr(d, core)
-            tr[d] = RemoteDMATransfer(dst_ids=[DstId(rid=rid, pnc=pid)], dma_engine_mask=_mask(eng[d]),
-                                      remote_sem=sem[("on%d" if d in near else "off%d") % c],
-                                      src=T["own%d" % c][:], dst=T["land%d" % c][:, slot * w:slot * w + w])
-            sent += len(eng[d])
+            return DstId(rid=rid, pnc=pid), T["land%d" % c][:, slot * step:slot * step + w]
+
+        fp, (nid, ndst) = [place(d) for d in far], place(near[0])
+        tr = [RemoteDMATransfer(dst_ids=[i for i, _ in fp], dma_engine_mask=_mask(far_e), remote_sem=sem["off%d" % c],
+                                srcs=[T["own%d" % c][:]], dsts=[p for _, p in fp]),
+              RemoteDMATransfer(dst_ids=[nid], dma_engine_mask=_mask(near_e), remote_sem=sem["on%d" % c],
+                                src=T["own%d" % c][:], dst=ndst)]
+        sent += len(far_e) + len(near_e)
         g.wait_ge(sem["a%d" % c], w)
-        if c == 0 and SPLIT_FIRST:
-            g.remote_dma_fused([tr[d] for d in far], local_sem=sem.sent)
-            g.remote_dma_fused([tr[d] for d in near], local_sem=sem.sent)
-        else:
-            g.remote_dma_fused([tr[d] for d in far + near], local_sem=sem.sent)
+        g.remote_dma_fused(tr, local_sem=sem.sent)
 
     Y.wait_ge(sem.sent, sent)
     Y.dma_start(T.w2b[:], T.w2[:]).then_inc(sem.lsecond, 16)
 
-    vc = [0]
+    vc, sc = [0], [0]
 
     def vstep(ins):
         ins.then_inc(sem.vc, 1)
         vc[0] += 1
 
-    shift = float(numpy.float32(EPS)) * (N * NC)
-    for c, (a, b) in enumerate(CHUNKS):
-        w = b - a
-        own, pre, prn, fr, tot, rec, land = (T["%s%d" % (n, c)] for n in ("own", "pre", "prn", "far", "tot", "rec", "land"))
-        V.wait_ge(sem["a%d" % c], w)
-        vstep(V.tensor_scalar(pre[:], own[:], shift, None, OP.add))
-        V.wait_ge(sem["on%d" % c], n_on)
-        V.wait_ge(sem.vc, vc[0])
-        vstep(V.tensor_tensor(prn[:], pre[:], land[:, 0:w], OP.add))
-        V.wait_ge(sem["off%d" % c], n_off)
-        vstep(V.tensor_tensor(fr[:], land[:, w:2 * w], land[:, 2 * w:3 * w], OP.add))
-        V.wait_ge(sem.vc, vc[0])
-        vstep(V.tensor_tensor(tot[:], fr[:], prn[:], OP.add))
-        V.wait_ge(sem.vc, vc[0])
-        V.reciprocal(rec[:], tot[:]).then_inc(sem["r%d" % c], 1)
-        S.wait_ge(sem["r%d" % c], 1)
-        S.activation(T["s%d" % c][:], rec[:], AF.Sqrt, scale=float(N * NC)).then_inc(sem["sd%d" % c], 1)
+    def sstep(ins):
+        ins.then_inc(sem.sc, 1)
+        sc[0] += 1
 
-    for i in range(G):
-        c, j = chunk_of(i)
-        col, out = T["s%d" % c][:, j:j + 1], T.hb[:, i:TW:4]
-        if i < G // 2:
-            V.wait_ge(sem["sd%d" % c], 1)
-            V.tensor_scalar(out, zb(i), col, None, OP.mult).then_inc(sem.nV, 1)
-        else:
-            S.wait_ge(sem["sd%d" % c], 1)
-            S.activation(out, zb(i), AF.Identity, scale=col).then_inc(sem.nS, 1)
-    V.wait_ge(sem.nV, G // 2)
-    V.wait_ge(sem.nS, G - G // 2)
+    shift = float(numpy.float32(EPS)) * (N * NC)
+    V.wait_ge(sem.a0, 1)
+    vstep(V.tensor_scalar(T.pre0[:], T.own0[:], shift, None, OP.add))
+    V.wait_ge(sem.vc, vc[0])
+    V.reciprocal(T.ra[:], T.pre0[:]).then_inc(sem.ra, 1)
+    V.wait_ge(sem.a1, W1)
+    vstep(V.tensor_scalar(T.land1[:, (N - 1) * BLK:(N - 1) * BLK + W1], T.own1[:], shift, None, OP.add))
+    S.wait_ge(sem.ra, 1)
+    sstep(S.activation(T.u[:], T.ra[:], AF.Sqrt, scale=float(N * NC)))
+
+    V.wait_ge(sem.on0, n_on)
+    V.wait_ge(sem.vc, vc[0])
+    vstep(V.tensor_tensor(T.prn0[:], T.pre0[:], T.land0[:, 0:1], OP.add))
+    V.wait_ge(sem.off0, n_off)
+    vstep(V.tensor_tensor(T.far0[:], T.land0[:, 1:2], T.land0[:, 2:3], OP.add))
+    V.wait_ge(sem.vc, vc[0])
+    vstep(V.tensor_tensor(T.tot0[:], T.far0[:], T.prn0[:], OP.add))
+    V.wait_ge(sem.vc, vc[0])
+    V.reciprocal(T.rec0[:], T.tot0[:]).then_inc(sem.r0, 1)
+    S.wait_ge(sem.r0, 1)
+    S.wait_ge(sem.sc, sc[0])
+    sstep(S.activation(T.v[:], T.rec0[:], AF.Sqrt, scale=T.pre0[:]))
+    S.wait_ge(sem.sc, sc[0])
+    sstep(S.activation(T.s0[:], T.v[:], AF.Identity, scale=T.u[:]))
+    S.wait_ge(sem.sc, sc[0])
+    S.activation(T.hb[:, 0:TW:4], zb(0), AF.Identity, scale=T.s0[:]).then_inc(sem.nS, 1)
+
+    V.wait_ge(sem.on1, n_on)
+    V.wait_ge(sem.off1, n_off)
+    for j in range(W1):
+        vstep(V.tensor_reduce(T.tot1[:, j:j + 1], T.land1[:, j:N * BLK:BLK], AxisListType.X, OP.add))
+    V.wait_ge(sem.vc, vc[0])
+    V.reciprocal(T.rec1[:], T.tot1[:]).then_inc(sem.r1, 1)
+    S.wait_ge(sem.r1, 1)
+    S.activation(T.s1[:], T.rec1[:], AF.Sqrt, scale=float(N * NC)).then_inc(sem.sd, 1)
+
+    HC = NC // 2
+    V.wait_ge(sem.sd, 1)
+    V.tensor_scalar(T.hb[:, 3:4 * HC:4], T.z[:, 512 * 3:512 * 3 + HC], T.s1[:, 2:3], None, OP.mult).then_inc(sem.h3a, 1)
+    V.tensor_scalar(T.hb[:, 1:TW:4], zb(1), T.s1[:, 0:1], None, OP.mult).then_inc(sem.nV, 1)
+    S.wait_ge(sem.sd, 1)
+    S.activation(T.hb[:, 2:TW:4], zb(2), AF.Identity, scale=T.s1[:, 1:2]).then_inc(sem.nS, 1)
+    S.wait_ge(sem.h3a, 1)
+    S.activation(T.hb[:, 4 * HC + 3:TW:4], T.z[:, 512 * 3 + HC:512 * 3 + NC], AF.Identity,
+                 scale=T.s1[:, 2:3]).then_inc(sem.nS, 1)
+    V.wait_ge(sem.h3a, 1)
+    V.wait_ge(sem.nV, 1)
+    V.wait_ge(sem.nS, 3)
     V.quantize_mx(T.qh[:], T.sh[:], T.hb[:]).then_inc(sem.vh, 1)
 
     dst, src = cores[(rank - 1) % N], cores[(rank + 1) % N]
     rid, pid = topo.addr(dst, core)
     m = topo.mask(core, dst)
     g.wait_ge(sem.vh, 1)
-    g.remote_dma(T.qr[:].bitcast(dt.uint8), T.qh[:].bitcast(dt.uint8), sem.harr, sem.sentH, pid, rid, m)
-    g.remote_dma(T.sr[:], T.sh[:], sem.harr, sem.sentH, pid, rid, m)
+    g.remote_dma(T.qr[:].bitcast(dt.uint8), T.qh[:].bitcast(dt.uint8), sem.harr, sem.sentC, pid, rid, m)
+    g.remote_dma(T.sr[:], T.sh[:], sem.harr, sem.sentS, pid, rid, m)
 
     V.wait_ge(sem.lsecond, 16)
     for t in range(2):
@@ -169,9 +194,10 @@ def rank_program(g, core, T, topo):
     V.tensor_copy(T.yb[:], T.yp[:, 0:NC]).then_inc(sem.yc, 1)
 
     Y.wait_ge(sem.vh, 1)
-    Y.wait_ge(sem.sentH, 2 * len(_bits(m)))
+    Y.wait_ge(sem.sentC, len(_bits(m)))
     Y.dma_start(T.h[:], T.hb[:]).then_inc(sem.sth, 16)
     Y.wait_ge(sem.yc, 1)
     Y.dma_start(T.y[:], T.yb[:]).then_inc(sem.sty, 16)
+    Y.wait_ge(sem.sentS, len(_bits(m)))
     Y.wait_ge(sem.sth, 16)
     Y.wait_ge(sem.sty, 16)

import numpy
from concourse.bass import DstId, RemoteDMATransfer
from concourse.mybir import dt, AluOpType, AxisListType, ActivationFunctionType

N, NC, G, EPS = 4, 128, 4, 0.001
TW = 4 * NC
CHUNKS = ((0, 1), (1, 4))
LOADS = ((0, 1), (1, 3), (3, 4))
BLK = 4

F32, BF16, CODE, U8 = "float32", "bfloat16", "float8_e4m3fn_x4", "uint8"
SCRATCH = {
    "xb": ("sbuf", [128, TW], BF16), "qx": ("sbuf", [128, NC], CODE), "sx": ("sbuf", [128, NC], U8),
    "w1b": ("sbuf", [128, G * TW], BF16), "qw1": ("sbuf", [128, G * NC], CODE), "sw1": ("sbuf", [128, G * NC], U8),
    "w2b": ("sbuf", [128, 2 * TW], BF16), "qw2": ("sbuf", [128, 2 * NC], CODE), "sw2": ("sbuf", [128, 2 * NC], U8),
    "hb": ("sbuf", [128, TW], BF16), "qh": ("sbuf", [128, NC], CODE), "sh": ("sbuf", [128, NC], U8),
    "qr": ("sbuf", [128, NC], CODE), "sr": ("sbuf", [128, NC], U8),
    "sq": ("sbuf", [128, G * NC], F32),
    "yb": ("sbuf", [128, NC], F32),
    "ra": ("sbuf", [128, 1], F32), "u": ("sbuf", [128, 1], F32), "v": ("sbuf", [128, 1], F32),
    "pre0": ("sbuf", [128, 1], F32), "prn0": ("sbuf", [128, 1], F32), "far0": ("sbuf", [128, 1], F32),
    "land0": ("sbuf", [128, N - 1], F32),
    "land1": ("sbuf", [128, N * BLK], F32),
    "z": ("psum", [128, G * 512], F32), "yp": ("psum", [128, 512], F32),
}
SEMAPHORES = ["lx", "lsecond", "vx", "vsecond", "vc", "nS", "nV", "vh", "harr", "my", "yc", "sth", "sty", "sent",
              "sentC", "sentS", "ra", "sc", "h3a", "sd"]
for _k in range(len(LOADS)):
    SEMAPHORES.append("lfirst%d" % _k)
for _i in range(G):
    SEMAPHORES += ["vw%d" % _i, "mm%d" % _i]
for _c, (_a, _b) in enumerate(CHUNKS):
    for _n in ("own", "tot", "rec", "s"):
        SCRATCH["%s%d" % (_n, _c)] = ("sbuf", [128, _b - _a], F32)
    SEMAPHORES += ["a%d" % _c, "on%d" % _c, "off%d" % _c, "r%d" % _c]


def _bits(m):
    return [e for e in range(m.bit_length()) if (m >> e) & 1]


def _mask(es):
    return sum(1 << e for e in es)


def _peers(c, cores, topo):
    o = [d for d in cores if d != c]
    near = [d for d in o if topo.host(d) == topo.host(c) and topo.chip(d) == topo.chip(c)]
    return near, [d for d in o if d not in near]


def rank_program(g, core, T, topo):
    rank = T.rank_of(core)
    if rank is None:
        return
    V, S, P, Y, sem = g.vector, g.scalar, g.tensor, g.sync, T.sem
    AF, OP = ActivationFunctionType, AluOpType
    cores = list(T.cores)
    near, far = _peers(core, cores, topo)
    far.sort(key=lambda d: d in _peers(cores[(cores.index(d) - 1) % N], cores, topo)[0])
    far_e = _bits(topo.mask(core, far[0]))
    near_e = [e for e in _bits(topo.mask(core, near[0])) if e not in far_e]
    n_on, n_off = len(near_e), len(far_e) * len(far)
    W1 = CHUNKS[1][1] - CHUNKS[1][0]

    def zb(i):
        return T.z[:, 512 * i:512 * i + NC]

    def chunk_of(i):
        for c, (a, b) in enumerate(CHUNKS):
            if a <= i < b:
                return c, i - a

    Y.dma_start(T.xb[:], T.x[:]).then_inc(sem.lx, 16)
    for k, (a, b) in enumerate(LOADS):
        Y.dma_start(T.w1b[:, TW * a:TW * b], T.w1[:, TW * a:TW * b]).then_inc(sem["lfirst%d" % k], 16)

    V.wait_ge(sem.lx, 16)
    V.quantize_mx(T.qx[:], T.sx[:], T.xb[:]).then_inc(sem.vx, 1)
    P.wait_ge(sem.vx, 1)
    for k, (a, b) in enumerate(LOADS):
        V.wait_ge(sem["lfirst%d" % k], 16)
        for i in range(a, b):
            V.quantize_mx(T.qw1[:, NC * i:NC * i + NC], T.sw1[:, NC * i:NC * i + NC],
                          T.w1b[:, TW * i:TW * i + TW]).then_inc(sem["vw%d" % i], 1)
            P.wait_ge(sem["vw%d" % i], 1)
            P.matmul_mx(zb(i), T.qw1[:, NC * i:NC * i + NC], T.sw1[:, NC * i:NC * i + NC], T.qx[:], T.sx[:],
                        True, True).then_inc(sem["mm%d" % i], 1)
            c, j = chunk_of(i)
            S.wait_ge(sem["mm%d" % i], 1)
            S.activation(T.sq[:, NC * i:NC * i + NC], zb(i), AF.Square,
                         accum_out=T["own%d" % c][:, j:j + 1]).then_inc(sem["a%d" % c], 1)

    sent = 0
    for c, (a, b) in enumerate(CHUNKS):
        w = b - a
        step = w if c == 0 else BLK

        def place(d):
            dn, df = _peers(d, cores, topo)
            slot = (dn + df).index(core)
            rid, pid = topo.addr(d, core)
            return DstId(rid=rid, pnc=pid), T["land%d" % c][:, slot * step:slot * step + w]

        fp, (nid, ndst) = [place(d) for d in far], place(near[0])
        tr = [RemoteDMATransfer(dst_ids=[i for i, _ in fp], dma_engine_mask=_mask(far_e), remote_sem=sem["off%d" % c],
                                srcs=[T["own%d" % c][:]], dsts=[p for _, p in fp]),
              RemoteDMATransfer(dst_ids=[nid], dma_engine_mask=_mask(near_e), remote_sem=sem["on%d" % c],
                                src=T["own%d" % c][:], dst=ndst)]
        sent += len(far_e) + len(near_e)
        g.wait_ge(sem["a%d" % c], w)
        g.remote_dma_fused(tr, local_sem=sem.sent)

    Y.wait_ge(sem.sent, sent)
    Y.dma_start(T.w2b[:], T.w2[:]).then_inc(sem.lsecond, 16)

    vc, sc = [0], [0]

    def vstep(ins):
        ins.then_inc(sem.vc, 1)
        vc[0] += 1

    def sstep(ins):
        ins.then_inc(sem.sc, 1)
        sc[0] += 1

    shift = float(numpy.float32(EPS)) * (N * NC)
    V.wait_ge(sem.a0, 1)
    vstep(V.tensor_scalar(T.pre0[:], T.own0[:], shift, None, OP.add))
    V.wait_ge(sem.vc, vc[0])
    V.reciprocal(T.ra[:], T.pre0[:]).then_inc(sem.ra, 1)
    V.wait_ge(sem.a1, W1)
    vstep(V.tensor_scalar(T.land1[:, (N - 1) * BLK:(N - 1) * BLK + W1], T.own1[:], shift, None, OP.add))
    S.wait_ge(sem.ra, 1)
    sstep(S.activation(T.u[:], T.ra[:], AF.Sqrt, scale=float(N * NC)))

    V.wait_ge(sem.on0, n_on)
    V.wait_ge(sem.vc, vc[0])
    vstep(V.tensor_tensor(T.prn0[:], T.pre0[:], T.land0[:, 0:1], OP.add))
    V.wait_ge(sem.off0, n_off)
    vstep(V.tensor_tensor(T.far0[:], T.land0[:, 1:2], T.land0[:, 2:3], OP.add))
    V.wait_ge(sem.vc, vc[0])
    vstep(V.tensor_tensor(T.tot0[:], T.far0[:], T.prn0[:], OP.add))
    V.wait_ge(sem.vc, vc[0])
    V.reciprocal(T.rec0[:], T.tot0[:]).then_inc(sem.r0, 1)
    S.wait_ge(sem.r0, 1)
    S.wait_ge(sem.sc, sc[0])
    sstep(S.activation(T.v[:], T.rec0[:], AF.Sqrt, scale=T.pre0[:]))
    S.wait_ge(sem.sc, sc[0])
    sstep(S.activation(T.s0[:], T.v[:], AF.Identity, scale=T.u[:]))
    S.wait_ge(sem.sc, sc[0])
    S.activation(T.hb[:, 0:TW:4], zb(0), AF.Identity, scale=T.s0[:]).then_inc(sem.nS, 1)

    V.wait_ge(sem.on1, n_on)
    V.wait_ge(sem.off1, n_off)
    for j in range(W1):
        vstep(V.tensor_reduce(T.tot1[:, j:j + 1], T.land1[:, j:N * BLK:BLK], AxisListType.X, OP.add))
    V.wait_ge(sem.vc, vc[0])
    V.reciprocal(T.rec1[:], T.tot1[:]).then_inc(sem.r1, 1)
    S.wait_ge(sem.r1, 1)
    S.activation(T.s1[:], T.rec1[:], AF.Sqrt, scale=float(N * NC)).then_inc(sem.sd, 1)

    HC = NC // 2
    V.wait_ge(sem.sd, 1)
    V.tensor_scalar(T.hb[:, 3:4 * HC:4], T.z[:, 512 * 3:512 * 3 + HC], T.s1[:, 2:3], None, OP.mult).then_inc(sem.h3a, 1)
    V.tensor_scalar(T.hb[:, 1:TW:4], zb(1), T.s1[:, 0:1], None, OP.mult).then_inc(sem.nV, 1)
    S.wait_ge(sem.sd, 1)
    S.activation(T.hb[:, 2:TW:4], zb(2), AF.Identity, scale=T.s1[:, 1:2]).then_inc(sem.nS, 1)
    S.wait_ge(sem.h3a, 1)
    S.activation(T.hb[:, 4 * HC + 3:TW:4], T.z[:, 512 * 3 + HC:512 * 3 + NC], AF.Identity,
                 scale=T.s1[:, 2:3]).then_inc(sem.nS, 1)
    V.wait_ge(sem.h3a, 1)
    V.wait_ge(sem.nV, 1)
    V.wait_ge(sem.nS, 3)
    V.quantize_mx(T.qh[:], T.sh[:], T.hb[:]).then_inc(sem.vh, 1)

    dst, src = cores[(rank - 1) % N], cores[(rank + 1) % N]
    rid, pid = topo.addr(dst, core)
    m = topo.mask(core, dst)
    g.wait_ge(sem.vh, 1)
    g.remote_dma(T.qr[:].bitcast(dt.uint8), T.qh[:].bitcast(dt.uint8), sem.harr, sem.sentC, pid, rid, m)
    g.remote_dma(T.sr[:], T.sh[:], sem.harr, sem.sentS, pid, rid, m)

    V.wait_ge(sem.lsecond, 16)
    for t in range(2):
        V.quantize_mx(T.qw2[:, NC * t:NC * t + NC], T.sw2[:, NC * t:NC * t + NC],
                      T.w2b[:, TW * t:TW * t + TW]).then_inc(sem.vsecond, 1)
    P.wait_ge(sem.vh, 1)
    P.wait_ge(sem.vsecond, 2)
    P.matmul_mx(T.yp[:, 0:NC], T.qw2[:, 0:NC], T.sw2[:, 0:NC], T.qh[:], T.sh[:], True, False)
    P.wait_ge(sem.harr, 2 * len(_bits(topo.mask(src, core))))
    P.matmul_mx(T.yp[:, 0:NC], T.qw2[:, NC:2 * NC], T.sw2[:, NC:2 * NC], T.qr[:], T.sr[:], False, True).then_inc(sem.my, 1)
    V.wait_ge(sem.my, 1)
    V.tensor_copy(T.yb[:], T.yp[:, 0:NC]).then_inc(sem.yc, 1)

    Y.wait_ge(sem.vh, 1)
    Y.wait_ge(sem.sentC, len(_bits(m)))
    Y.dma_start(T.h[:], T.hb[:]).then_inc(sem.sth, 16)
    Y.wait_ge(sem.yc, 1)
    Y.dma_start(T.y[:], T.yb[:]).then_inc(sem.sty, 16)
    Y.wait_ge(sem.sentS, len(_bits(m)))
    Y.wait_ge(sem.sth, 16)
    Y.wait_ge(sem.sty, 16)
